import numpy as np
import ml_dtypes


def mxq(x, axis, fmt="e4m3"):
    dtype, down = {"e4m3": (ml_dtypes.float8_e4m3fn, 7), "e5m2": (ml_dtypes.float8_e5m2, 14)}[fmt]
    v = np.moveaxis(np.asarray(x, np.float32).astype(ml_dtypes.bfloat16).astype(np.float64), axis, -1)
    blocks = v.reshape(v.shape[:-1] + (-1, 32))
    amax = np.abs(blocks).max(-1, keepdims=True)
    byte = np.maximum(np.where(amax > 0, np.frexp(amax)[1] - 1 + 127, 0) - down, 1)
    scale = np.exp2(byte - 127.0)
    codes = (blocks / scale).astype(np.float32).astype(dtype).astype(np.float64)
    return np.moveaxis((codes * scale).reshape(v.shape), -1, axis)


WIDE = False


def mx_kscale(k):
    if not WIDE:
        return np.ones(k)
    levels = np.array([10, -10, 5, -5, 0])
    if k % 512:
        return np.exp2(np.random.permutation(np.resize(levels, k // 32))).repeat(32)
    a = np.empty((k // 512, 16))
    for p in range(k // 512):
        a[p, :8] = np.random.permutation(np.resize(levels, 8))
        for g in range(8):
            far = levels[np.abs(levels - a[p, g]) >= 10]
            a[p, g + 8] = far[np.random.randint(len(far))]
    return np.exp2(a.ravel()).repeat(32)


def f64(x):
    return np.asarray(x).astype(np.float64)


def striped(idx):
    return np.tile(np.asarray(idx).reshape(-1, 16).T, (8, 1)).astype(np.uint16)


def unstriped(offs):
    return offs[:16].T.reshape(-1).astype(np.int64)


def striped8(idx):
    return np.asarray(idx).reshape(8, -1, 16).transpose(0, 2, 1).reshape(128, -1).astype(np.uint16)


def unstriped8(offs):
    return offs.reshape(8, 16, -1).transpose(0, 2, 1).reshape(8, -1).astype(np.int64)


def pick8(x, idx, run):
    r = np.arange(len(x))
    return x[r[:, None], idx[r % (8 * run) // run]]


E2M1 = np.array([0.0, 0.5, 1.0, 1.5, 2.0, 3.0, 4.0, 6.0, -0.0, -0.5, -1.0, -1.5, -2.0, -3.0, -4.0, -6.0])


def pack_weight(w, fmt):
    k, n = w.shape
    w = f64(np.asarray(w, np.float32).astype(ml_dtypes.bfloat16)).reshape(k // 32, 32, n)
    amax = np.abs(w).max(1)
    if fmt == "e4m3":
        byte = np.frexp(amax)[1] - 1 + 127 - 7
    else:
        mant, ex = np.frexp(amax / 6.0)
        byte = np.where(mant > 0.5, ex, ex - 1) + 127
    byte = np.clip(np.where(amax > 0, byte, 1), 1, 254)
    scaled = (w * np.exp2(127.0 - byte)[:, None, :]).reshape(k, n).astype(np.float32)
    by_word = np.ascontiguousarray(scaled.reshape(k // 512, 128, 4, n).transpose(0, 1, 3, 2))
    if fmt == "e4m3":
        words = by_word.astype(ml_dtypes.float8_e4m3fn).view(np.uint8)
    else:
        c = by_word.astype(ml_dtypes.float4_e2m1fn).view(np.uint8) & 0xF
        words = (c[..., 0::2] | (c[..., 1::2] << 4)).reshape(k // 512, 128, 2 * n)
    return np.ascontiguousarray(words), np.ascontiguousarray(byte.astype(np.uint8).reshape(k // 512, 16, n))


def unpack_weight(words, scales, fmt):
    g, _, n = scales.shape
    words = np.ascontiguousarray(words).reshape(g, 128, n, -1)
    if fmt == "e4m3":
        vals = words.view(ml_dtypes.float8_e4m3fn).astype(np.float64)
    else:
        nib = np.empty((g, 128, n, 4), np.uint8)
        nib[..., 0::2] = words & 0xF
        nib[..., 1::2] = words >> 4
        vals = E2M1[nib]
    vals = vals * np.repeat(np.exp2(scales.astype(np.float64) - 127.0), 8, axis=1)[..., None]
    return vals.transpose(0, 1, 3, 2).reshape(g * 512, n)


K, R, F, T, J, U = 512, 128, 512, 2048, 512, 1024


def setup_inputs():
    n = np.random.standard_normal
    idx = np.random.permutation(T)[:J]
    idx2 = np.stack([np.random.permutation(U)[:J] for _ in range(8)])
    fk = mx_kscale(K)
    ff = mx_kscale(F)
    fj = mx_kscale(J)
    tj = np.ones(T)
    tj[idx] = fj
    tabp = pack_weight(n((K, T)) / fk[:, None], "e2m1")
    return {
        "tab_words": tabp[0],
        "tab_scales": tabp[1],
        "w1": (n((K, R)) * 1 / np.sqrt(K) * fk[:, None]).astype(np.float32),
        "gain": (np.random.uniform(0.5, 1.5, (R, 1))).astype(np.float32),
        "ground": (n((R, U)) * 0.7).astype(np.float32),
        "wo": (n((F, R)) * 1 / np.sqrt(F) * ff[:, None]).astype(np.float32),
        "dy": (n((F, U)) / ff[:, None]).astype(np.float32),
        "js": (np.random.uniform(0.5, 2.0, (1, J)) * fj).astype(np.float32),
        "xrows": (n((K, T)) / tj).astype(np.float32),
        "old": (n((K, R)) * 4.0).astype(np.float32),
        "offs": striped(idx),
        "offs2": striped8(idx2),
    }


def reference(tab_words, tab_scales, w1, gain, ground, wo, dy, js, xrows, old, offs, offs2):
    idx = unstriped(offs)
    idx2 = unstriped8(offs2)
    tabu = unpack_weight(tab_words, tab_scales, "e2m1")
    w1q = mxq(f64(w1), 0, "e4m3")
    tabidxg = tabu[:, idx]
    a = w1q.T @ tabidxg
    h1 = a * f64(gain)
    pg = np.zeros((R, U))
    pg[np.arange(R)[:, None], idx2[np.arange(R) % 128 // 16]] = h1
    s = pg + f64(ground)
    u1 = np.tanh(s)
    woq = mxq(f64(wo), 0, "e4m3")
    dyq = mxq(f64(dy), 0, "e4m3")
    c0 = woq.T @ dyq
    ds = c0 * (1.0 - np.square(u1))
    dh1 = pick8(ds, idx2, 16)
    da = dh1 * f64(gain)
    gs = da * f64(js)
    gt1 = gs.T
    xt = f64(xrows)[:, idx].T
    xtq = mxq(xt, 0, "e4m3")
    gt1q = mxq(gt1, 0, "e4m3")
    gw = xtq.T @ gt1q
    y = gw + f64(old)
    return y

@@ -1,0 +1,199 @@
+from contextlib import ExitStack
+
+import concourse.mybir as mybir
+from concourse.masks import make_identity
+
+K, R, F, T, J, U = 512, 128, 512, 2048, 512, 1024
+FLOPS = 2 * K * R * J + 2 * F * R * U + 2 * J * K * R
+
+F32 = mybir.dt.float32
+BF16 = mybir.dt.bfloat16
+I32 = mybir.dt.int32
+U32 = mybir.dt.uint32
+U16 = mybir.dt.uint16
+U8 = mybir.dt.uint8
+FP8X4 = mybir.dt.float8_e4m3fn_x4
+FP4X4 = mybir.dt.float4_e2m1fn_x4
+ACT = mybir.ActivationFunctionType
+ALU = mybir.AluOpType
+
+P = 128
+PACK = 4
+HALF = U // 2
+
+
+def interleave(nc, grouped, raw, scale):
+    nc.scalar.activation(
+        out=grouped.rearrange("p (c i) t -> p c t i", i=4),
+        in_=raw.rearrange("p t (c i) -> p c t i", i=4),
+        func=ACT.Copy,
+        scale=scale,
+    )
+
+
+def quantize(nc, codes, scales, grouped):
+    nc.vector.quantize_mx(out=codes.bitcast(FP8X4), scales=scales, in_=grouped)
+
+
+def tile_attend_cpageput_w_kernel(tc, tab_words, tab_scales, w1, gain, ground, wo, dy, js, xrows, old, offs, offs2, out):
+    nc = tc.nc
+    with ExitStack() as ctx:
+        sb = ctx.enter_context(tc.tile_pool(name="sb", bufs=1))
+        ps = ctx.enter_context(tc.psum_pool(name="ps", bufs=1))
+
+        def tile(name, shape, dtype, on=None):
+            return sb.tile(shape, dtype, name=name, tag=on or name, align_bytes=64)
+
+        offs_t = sb.tile([P, J // 16], U16, name="offs_t")
+        offs2_t = sb.tile([P, J // 16], U16, name="offs2_t")
+        tab_w = tile("tab_w", [P, T], U16)
+        tab_s = tile("tab_s", [P, T], U8)
+        w1_raw = tile("w1_raw", [P, PACK, R], F32)
+        wo_raw = tile("wo_raw", [P, PACK, R], F32)
+        gain_t = tile("gain_t", [P, 1], F32)
+        js_t = tile("js_t", [P, PACK], F32)
+        ground_t = tile("ground_t", [P, U], F32)
+        dy_cuts = [(0, 256), (256, 512), (512, 1024)]
+        dy_raw = [tile("dy_raw%d" % i, [P, PACK, b - a], F32) for i, (a, b) in enumerate(dy_cuts)]
+        x_raw = [tile("x_raw%d" % t, [P, T], F32) for t in range(PACK)]
+        old_t = tile("old_t", [P, PACK, R], F32)
+        ident = tile("ident", [P, P], F32)
+        page = tile("page", [P, U], F32)
+
+        nc.vector.memset(tab_s[:].bitcast(I32), 0)
+        nc.vector.memset(page[:], 0.0)
+        nc.gpsimd.dma_start(out=gain_t[:], in_=gain)
+        nc.gpsimd.dma_start(out=js_t[:], in_=js.rearrange("o (q t) -> (o q) t", t=PACK))
+        make_identity(nc, ident[:])
+
+        x_planes = xrows.rearrange("(p t) c -> p t c", t=PACK)
+        dy_rows = dy.rearrange("(p t) u -> p t u", t=PACK)
+        nc.sync.dma_start(out=tab_w[:].bitcast(I32), in_=tab_words[0].bitcast(I32))
+        for i in range(4):
+            nc.sync.dma_start(out=tab_s[i:P:32, :].bitcast(I32), in_=tab_scales[0, i:16:4, :].bitcast(I32))
+        nc.sync.dma_start(offs_t[:], offs)
+        nc.sync.dma_start(out=w1_raw[:], in_=w1.rearrange("(p t) r -> p t r", t=PACK))
+        nc.sync.dma_start(out=dy_raw[0][:], in_=dy_rows[:, :, 0:256])
+        nc.sync.dma_start(offs2_t[:], offs2)
+        nc.sync.dma_start(out=wo_raw[:], in_=wo.rearrange("(p t) r -> p t r", t=PACK))
+        nc.sync.dma_start(out=dy_raw[1][:], in_=dy_rows[:, :, 256:512])
+        nc.sync.dma_start(out=dy_raw[2][:], in_=dy_rows[:, :, 512:1024])
+        nc.sync.dma_start(out=ground_t[:], in_=ground)
+        for t in range(PACK):
+            nc.sync.dma_start(out=x_raw[t][:], in_=x_planes[:, t, :])
+        nc.sync.dma_start(out=old_t[:], in_=old.rearrange("(p t) r -> p t r", t=PACK))
+
+        JH = J // 2
+        w1_b = tile("w1_b", [P, R, PACK], BF16)
+        w1_c = tile("w1_c", [P, R], U32)
+        w1_s = tile("w1_s", [P, R], U8)
+        dy_b = [tile("dy_b%d" % h, [P, HALF, PACK], BF16) for h in range(2)]
+        interleave(nc, w1_b[:], w1_raw[:], 1.0)
+        a_ps = ps.tile([P, J], F32, name="a_ps")
+        h1 = []
+        for h in range(2):
+            lst = slice(h * JH // 16, (h + 1) * JH // 16)
+            tabg_w = tile("tabg_w%d" % h, [P, JH], U16, on="w1_b" if h else None)
+            tabg_s = tile("tabg_s%d" % h, [P, JH], U8)
+            nc.vector.tensor_copy(tabg_w[:], tab_w[:].indirect(offs_t[:, lst]))
+            nc.vector.tensor_copy(tabg_s[:], tab_s[:].indirect(offs_t[:, lst]))
+            if h == 0:
+                quantize(nc, w1_c[:], w1_s[:], w1_b[:].rearrange("p r t -> p (r t)"))
+            nc.tensor.matmul_mx(out=a_ps[:, h * JH : (h + 1) * JH], lhsT=w1_c[:].bitcast(FP8X4), lhsT_scale=w1_s[:],
+                                rhs=tabg_w[:].bitcast(FP4X4), rhs_scale=tabg_s[:], start=True, stop=True)
+            h1.append(tile("h1_%d" % h, [P, JH], F32, on="dy_raw0" if h else None))
+            nc.scalar.activation(out=h1[h][:], in_=a_ps[:, h * JH : (h + 1) * JH], func=ACT.Copy, scale=gain_t[:])
+            if h == 0:
+                interleave(nc, dy_b[0][:, 0:256, :], dy_raw[0][:], 1.0)
+        for h in range(2):
+            lst = slice(h * JH // 16, (h + 1) * JH // 16)
+            nc.vector.tensor_copy(page[:].indirect(offs2_t[:, lst]), h1[h][:])
+
+        x_c = {}
+        x_s = [tile("x_s%d" % t, [P, P], U8) for t in range(PACK)]
+        x_b = [tile("x_b%d" % t, [P, P * PACK], BF16) for t in range(PACK)]
+
+        def gather_x(t):
+            xg = tile("xg%d" % t, [P, J], BF16)
+            nc.vector.tensor_copy(xg[:], x_raw[t][:].indirect(offs_t[:]))
+            words = xg[:].bitcast(F32)
+            xt_ps = ps.tile([P, 2, P], F32, name="xt_ps", tag="xt_ps%d" % (t % 2))
+            for u in range(2):
+                nc.tensor.transpose(xt_ps[:, u, :], words[:, u : J // 2 : 2], ident[:])
+            nc.scalar.copy(out=x_b[t][:].bitcast(F32).rearrange("q (k u) -> q k u", u=2),
+                           in_=xt_ps[:].rearrange("q u k -> q k u"))
+
+        def quantize_x(t, on):
+            x_c[t] = tile("x_c%d" % t, [P, P], U32, on=on)
+            quantize(nc, x_c[t][:], x_s[t][:], x_b[t][:])
+
+        wo_b = tile("wo_b", [P, R, PACK], BF16)
+        wo_c = tile("wo_c", [P, R], U32)
+        wo_s = tile("wo_s", [P, R], U8)
+        interleave(nc, wo_b[:], wo_raw[:], -1.0)
+        quantize(nc, wo_c[:], wo_s[:], wo_b[:].rearrange("p r t -> p (r t)"))
+
+        ds = tile("ds", [P, U], F32)
+        s_t = [tile("s_t%d" % h, [P, HALF], F32) for h in range(2)]
+        sq = [tile("sq%d" % h, [P, HALF], F32) for h in range(2)]
+        c0 = [ps.tile([P, HALF], F32, name="c0_%d" % h) for h in range(2)]
+        interleave(nc, dy_b[0][:, 256:512, :], dy_raw[1][:], 1.0)
+        for q in range(2):
+            cols = slice(q * 256, (q + 1) * 256)
+            interleave(nc, dy_b[1][:, cols, :], dy_raw[2][:, :, cols], 1.0)
+        for h in range(2):
+            cols = slice(h * HALF, (h + 1) * HALF)
+            nc.vector.tensor_tensor(s_t[h][:], page[:, cols], ground_t[:, cols], ALU.add)
+        for h in range(2):
+            u1 = tile("u1_%d" % h, [P, HALF], F32)
+            nc.scalar.activation(out=u1[:], in_=s_t[h][:], func=ACT.Tanh)
+            nc.scalar.activation(out=sq[h][:], in_=u1[:], func=ACT.Square)
+        for h in range(2):
+            dy_c = tile("dy_c%d" % h, [P, HALF], U32)
+            dy_s = tile("dy_s%d" % h, [P, HALF], U8)
+            quantize(nc, dy_c[:], dy_s[:], dy_b[h][:].rearrange("p u t -> p (u t)"))
+            nc.tensor.matmul_mx(out=c0[h][:], lhsT=wo_c[:].bitcast(FP8X4), lhsT_scale=wo_s[:],
+                                rhs=dy_c[:].bitcast(FP8X4), rhs_scale=dy_s[:], start=True, stop=True)
+        for h in range(2):
+            cols = slice(h * HALF, (h + 1) * HALF)
+            nc.vector.scalar_tensor_tensor(out=ds[:, cols], in0=sq[h][:], scalar=1.0, in1=c0[h][:],
+                                           op0=ALU.subtract, op1=ALU.mult)
+            if h == 0:
+                gather_x(0)
+        dh1 = tile("dh1", [P, J], F32)
+        nc.vector.tensor_copy(dh1[:], ds[:].indirect(offs2_t[:]))
+        da = tile("da", [P, PACK, P], F32)
+        nc.scalar.activation(out=da[:].rearrange("r t q -> r q t"), in_=dh1[:].rearrange("r (q t) -> r q t", t=PACK),
+                             func=ACT.Copy, scale=gain_t[:])
+        gt_ps = ps.tile([P, PACK, P], F32, name="gt_ps")
+        for t in range(PACK):
+            nc.tensor.transpose(gt_ps[:, t, :], da[:, t, :], ident[:])
+        gather_x(1)
+        quantize_x(0, "ds")
+        g_b = tile("g_b", [P, R, PACK], BF16)
+        g_c = tile("g_c", [P, R], U32)
+        g_s = tile("g_s", [P, R], U8)
+        nc.vector.tensor_tensor(g_b[:], gt_ps[:].rearrange("q t r -> q r t"),
+                                js_t[:].unsqueeze(1).to_broadcast([P, R, PACK]), ALU.mult)
+        quantize_x(1, None)
+        quantize(nc, g_c[:], g_s[:], g_b[:].rearrange("q r t -> q (r t)"))
+        gather_x(2)
+        gather_x(3)
+        quantize_x(2, "x_raw3")
+
+        out_rows = out.rearrange("(p t) r -> p t r", t=PACK)
+        gw_a = ps.tile([P, PACK - 1, R], F32, name="gw_a")
+        gw_b = ps.tile([P, 1, R], F32, name="gw_b")
+        y_a = tile("y_a", [P, PACK - 1, R], F32)
+        y_b = tile("y_b", [P, 1, R], F32)
+        for t in range(PACK - 1):
+            nc.tensor.matmul_mx(out=gw_a[:, t, :], lhsT=x_c[t][:].bitcast(FP8X4), lhsT_scale=x_s[t][:],
+                                rhs=g_c[:].bitcast(FP8X4), rhs_scale=g_s[:], start=True, stop=True)
+        nc.vector.tensor_tensor(y_a[:], gw_a[:], old_t[:, 0 : PACK - 1, :], ALU.add)
+        nc.sync.dma_start(out=out_rows[:, 0 : PACK - 1, :], in_=y_a[:])
+        t = PACK - 1
+        quantize_x(t, None)
+        nc.tensor.matmul_mx(out=gw_b[:, 0, :], lhsT=x_c[t][:].bitcast(FP8X4), lhsT_scale=x_s[t][:],
+                            rhs=g_c[:].bitcast(FP8X4), rhs_scale=g_s[:], start=True, stop=True)
+        nc.vector.tensor_tensor(y_b[:], gw_b[:], old_t[:, t : t + 1, :], ALU.add)
+        nc.sync.dma_start(out=out_rows[:, t : t + 1, :], in_=y_b[:])

@@ -53,7 +53,7 @@ def tile_attend_cpageput_w_kernel(tc, tab_words, tab_scales, w1, gain, ground, w
         gain_t = tile("gain_t", [P, 1], F32)
         js_t = tile("js_t", [P, PACK], F32)
         ground_t = tile("ground_t", [P, U], F32)
-        dy_cuts = [(0, 256), (256, 512), (512, 1024)]
+        dy_cuts = [(0, 256), (256, 512), (512, 768), (768, 1024)]
         dy_raw = [tile("dy_raw%d" % i, [P, PACK, b - a], F32) for i, (a, b) in enumerate(dy_cuts)]
         x_raw = [tile("x_raw%d" % t, [P, T], F32) for t in range(PACK)]
         old_t = tile("old_t", [P, PACK, R], F32)
@@ -68,132 +68,137 @@ def tile_attend_cpageput_w_kernel(tc, tab_words, tab_scales, w1, gain, ground, w
 
         x_planes = xrows.rearrange("(p t) c -> p t c", t=PACK)
         dy_rows = dy.rearrange("(p t) u -> p t u", t=PACK)
+        nc.sync.dma_start(offs_t[:], offs)
         nc.sync.dma_start(out=tab_w[:].bitcast(I32), in_=tab_words[0].bitcast(I32))
         for i in range(4):
             nc.sync.dma_start(out=tab_s[i:P:32, :].bitcast(I32), in_=tab_scales[0, i:16:4, :].bitcast(I32))
-        nc.sync.dma_start(offs_t[:], offs)
         nc.sync.dma_start(out=w1_raw[:], in_=w1.rearrange("(p t) r -> p t r", t=PACK))
+        nc.sync.dma_start(out=wo_raw[:], in_=wo.rearrange("(p t) r -> p t r", t=PACK))
         nc.sync.dma_start(out=dy_raw[0][:], in_=dy_rows[:, :, 0:256])
         nc.sync.dma_start(offs2_t[:], offs2)
-        nc.sync.dma_start(out=wo_raw[:], in_=wo.rearrange("(p t) r -> p t r", t=PACK))
         nc.sync.dma_start(out=dy_raw[1][:], in_=dy_rows[:, :, 256:512])
-        nc.sync.dma_start(out=dy_raw[2][:], in_=dy_rows[:, :, 512:1024])
+        nc.sync.dma_start(out=dy_raw[2][:], in_=dy_rows[:, :, 512:768])
+        nc.sync.dma_start(out=dy_raw[3][:], in_=dy_rows[:, :, 768:1024])
         nc.sync.dma_start(out=ground_t[:], in_=ground)
-        for t in range(PACK):
-            nc.sync.dma_start(out=x_raw[t][:], in_=x_planes[:, t, :])
+        nc.sync.dma_start(out=x_raw[0][:], in_=x_planes[:, 0, :])
+        nc.sync.dma_start(out=x_raw[1][:], in_=x_planes[:, 1, :])
+        nc.sync.dma_start(out=x_raw[2][:], in_=x_planes[:, 2, :])
+        nc.sync.dma_start(out=x_raw[3][:], in_=x_planes[:, 3, :])
         nc.sync.dma_start(out=old_t[:], in_=old.rearrange("(p t) r -> p t r", t=PACK))
-
-        JH = J // 2
         w1_b = tile("w1_b", [P, R, PACK], BF16)
+        interleave(nc, w1_b[:], w1_raw[:], 1.0)
+        wo_b = tile("wo_b", [P, R, PACK], BF16)
+        interleave(nc, wo_b[:], wo_raw[:], -1.0)
+        tabg_w0 = tile("tabg_w0", [P, 256], U16)
+        nc.vector.tensor_copy(tabg_w0[:], tab_w[:].indirect(offs_t[:, slice(0, 16)]))
+        tabg_s0 = tile("tabg_s0", [P, 256], U8)
+        nc.vector.tensor_copy(tabg_s0[:], tab_s[:].indirect(offs_t[:, slice(0, 16)]))
         w1_c = tile("w1_c", [P, R], U32)
         w1_s = tile("w1_s", [P, R], U8)
-        dy_b = [tile("dy_b%d" % h, [P, HALF, PACK], BF16) for h in range(2)]
-        interleave(nc, w1_b[:], w1_raw[:], 1.0)
-        a_ps = ps.tile([P, J], F32, name="a_ps")
-        h1 = []
-        for h in range(2):
-            lst = slice(h * JH // 16, (h + 1) * JH // 16)
-            tabg_w = tile("tabg_w%d" % h, [P, JH], U16, on="w1_b" if h else None)
-            tabg_s = tile("tabg_s%d" % h, [P, JH], U8)
-            nc.vector.tensor_copy(tabg_w[:], tab_w[:].indirect(offs_t[:, lst]))
-            nc.vector.tensor_copy(tabg_s[:], tab_s[:].indirect(offs_t[:, lst]))
-            if h == 0:
-                quantize(nc, w1_c[:], w1_s[:], w1_b[:].rearrange("p r t -> p (r t)"))
-            nc.tensor.matmul_mx(out=a_ps[:, h * JH : (h + 1) * JH], lhsT=w1_c[:].bitcast(FP8X4), lhsT_scale=w1_s[:],
-                                rhs=tabg_w[:].bitcast(FP4X4), rhs_scale=tabg_s[:], start=True, stop=True)
-            h1.append(tile("h1_%d" % h, [P, JH], F32, on="dy_raw0" if h else None))
-            nc.scalar.activation(out=h1[h][:], in_=a_ps[:, h * JH : (h + 1) * JH], func=ACT.Copy, scale=gain_t[:])
-            if h == 0:
-                interleave(nc, dy_b[0][:, 0:256, :], dy_raw[0][:], 1.0)
-        for h in range(2):
-            lst = slice(h * JH // 16, (h + 1) * JH // 16)
-            nc.vector.tensor_copy(page[:].indirect(offs2_t[:, lst]), h1[h][:])
-
-        x_c = {}
-        x_s = [tile("x_s%d" % t, [P, P], U8) for t in range(PACK)]
-        x_b = [tile("x_b%d" % t, [P, P * PACK], BF16) for t in range(PACK)]
-
-        def gather_x(t):
-            xg = tile("xg%d" % t, [P, J], BF16)
-            nc.vector.tensor_copy(xg[:], x_raw[t][:].indirect(offs_t[:]))
-            words = xg[:].bitcast(F32)
-            xt_ps = ps.tile([P, 2, P], F32, name="xt_ps", tag="xt_ps%d" % (t % 2))
-            for u in range(2):
-                nc.tensor.transpose(xt_ps[:, u, :], words[:, u : J // 2 : 2], ident[:])
-            nc.scalar.copy(out=x_b[t][:].bitcast(F32).rearrange("q (k u) -> q k u", u=2),
-                           in_=xt_ps[:].rearrange("q u k -> q k u"))
-
-        def quantize_x(t, on):
-            x_c[t] = tile("x_c%d" % t, [P, P], U32, on=on)
-            quantize(nc, x_c[t][:], x_s[t][:], x_b[t][:])
-
-        wo_b = tile("wo_b", [P, R, PACK], BF16)
+        quantize(nc, w1_c[:], w1_s[:], w1_b[:].rearrange("p r t -> p (r t)"))
+        a_ps0 = ps.tile([P, 256], F32, name="a_ps0", tag="a0")
+        nc.tensor.matmul_mx(out=a_ps0[:], lhsT=w1_c[:].bitcast(FP8X4), lhsT_scale=w1_s[:], rhs=tabg_w0[:].bitcast(FP4X4), rhs_scale=tabg_s0[:], start=True, stop=True)
+        h1_0 = tile("h1_0", [P, 256], F32)
+        nc.scalar.activation(out=h1_0[:], in_=a_ps0[:], func=ACT.Copy, scale=gain_t[:])
+        tabg_s1 = tile("tabg_s1", [P, 256], U8, on="w1_raw")
+        nc.vector.tensor_copy(tabg_s1[:], tab_s[:].indirect(offs_t[:, slice(16, 32)]))
+        tabg_w1 = tile("tabg_w1", [P, 256], U16, on="w1_b")
+        nc.vector.tensor_copy(tabg_w1[:], tab_w[:].indirect(offs_t[:, slice(16, 32)]))
+        a_ps1 = ps.tile([P, 256], F32, name="a_ps1", tag="a1")
+        nc.tensor.matmul_mx(out=a_ps1[:], lhsT=w1_c[:].bitcast(FP8X4), lhsT_scale=w1_s[:], rhs=tabg_w1[:].bitcast(FP4X4), rhs_scale=tabg_s1[:], start=True, stop=True)
+        h1_1 = tile("h1_1", [P, 256], F32)
+        nc.scalar.activation(out=h1_1[:], in_=a_ps1[:], func=ACT.Copy, scale=gain_t[:])
+        dy_b0 = tile("dy_b0", [P, HALF, PACK], BF16)
+        interleave(nc, dy_b0[:, 0:256, :], dy_raw[0][:], 1.0)
         wo_c = tile("wo_c", [P, R], U32)
         wo_s = tile("wo_s", [P, R], U8)
-        interleave(nc, wo_b[:], wo_raw[:], -1.0)
         quantize(nc, wo_c[:], wo_s[:], wo_b[:].rearrange("p r t -> p (r t)"))
-
-        ds = tile("ds", [P, U], F32)
-        s_t = [tile("s_t%d" % h, [P, HALF], F32) for h in range(2)]
-        sq = [tile("sq%d" % h, [P, HALF], F32) for h in range(2)]
-        c0 = [ps.tile([P, HALF], F32, name="c0_%d" % h) for h in range(2)]
-        interleave(nc, dy_b[0][:, 256:512, :], dy_raw[1][:], 1.0)
-        for q in range(2):
-            cols = slice(q * 256, (q + 1) * 256)
-            interleave(nc, dy_b[1][:, cols, :], dy_raw[2][:, :, cols], 1.0)
-        for h in range(2):
-            cols = slice(h * HALF, (h + 1) * HALF)
-            nc.vector.tensor_tensor(s_t[h][:], page[:, cols], ground_t[:, cols], ALU.add)
-        for h in range(2):
-            u1 = tile("u1_%d" % h, [P, HALF], F32)
-            nc.scalar.activation(out=u1[:], in_=s_t[h][:], func=ACT.Tanh)
-            nc.scalar.activation(out=sq[h][:], in_=u1[:], func=ACT.Square)
-        for h in range(2):
-            dy_c = tile("dy_c%d" % h, [P, HALF], U32)
-            dy_s = tile("dy_s%d" % h, [P, HALF], U8)
-            quantize(nc, dy_c[:], dy_s[:], dy_b[h][:].rearrange("p u t -> p (u t)"))
-            nc.tensor.matmul_mx(out=c0[h][:], lhsT=wo_c[:].bitcast(FP8X4), lhsT_scale=wo_s[:],
-                                rhs=dy_c[:].bitcast(FP8X4), rhs_scale=dy_s[:], start=True, stop=True)
-        for h in range(2):
-            cols = slice(h * HALF, (h + 1) * HALF)
-            nc.vector.scalar_tensor_tensor(out=ds[:, cols], in0=sq[h][:], scalar=1.0, in1=c0[h][:],
-                                           op0=ALU.subtract, op1=ALU.mult)
-            if h == 0:
-                gather_x(0)
+        nc.vector.tensor_copy(page[:].indirect(offs2_t[:, slice(0, 16)]), h1_0[:])
+        nc.vector.tensor_copy(page[:].indirect(offs2_t[:, slice(16, 32)]), h1_1[:])
+        interleave(nc, dy_b0[:, 256:512, :], dy_raw[1][:], 1.0)
+        dy_b1 = tile("dy_b1", [P, HALF, PACK], BF16)
+        interleave(nc, dy_b1[:, 0:256, :], dy_raw[2][:], 1.0)
+        interleave(nc, dy_b1[:, 256:512, :], dy_raw[3][:], 1.0)
+        dy_c0 = tile("dy_c0", [P, HALF], U32)
+        dy_s0 = tile("dy_s0", [P, HALF], U8)
+        quantize(nc, dy_c0[:], dy_s0[:], dy_b0[:].rearrange("p u t -> p (u t)"))
+        c0_0 = ps.tile([P, HALF], F32, name="c0_0", tag="c0")
+        nc.tensor.matmul_mx(out=c0_0[:], lhsT=wo_c[:].bitcast(FP8X4), lhsT_scale=wo_s[:], rhs=dy_c0[:].bitcast(FP8X4), rhs_scale=dy_s0[:], start=True, stop=True)
+        s_t0 = tile("s_t0", [P, HALF], F32)
+        nc.vector.tensor_tensor(s_t0[:], page[:, 0:512], ground_t[:, 0:512], ALU.add)
+        s_t1 = tile("s_t1", [P, HALF], F32)
+        nc.vector.tensor_tensor(s_t1[:], page[:, 512:1024], ground_t[:, 512:1024], ALU.add)
+        dy_c1 = tile("dy_c1", [P, HALF], U32)
+        dy_s1 = tile("dy_s1", [P, HALF], U8)
+        quantize(nc, dy_c1[:], dy_s1[:], dy_b1[:].rearrange("p u t -> p (u t)"))
+        c0_1 = ps.tile([P, HALF], F32, name="c0_1", tag="c1")
+        nc.tensor.matmul_mx(out=c0_1[:], lhsT=wo_c[:].bitcast(FP8X4), lhsT_scale=wo_s[:], rhs=dy_c1[:].bitcast(FP8X4), rhs_scale=dy_s1[:], start=True, stop=True)
+        u1 = tile("u1", [P, U], F32, on="dy_raw3")
+        nc.scalar.activation(out=u1[:, 0:512], in_=s_t0[:], func=ACT.Tanh)
+        nc.scalar.activation(out=u1[:, 512:1024], in_=s_t1[:], func=ACT.Tanh)
+        sq0 = tile("sq0", [P, HALF], F32)
+        nc.scalar.activation(out=sq0[:], in_=u1[:, 0:512], func=ACT.Square)
+        sq1 = tile("sq1", [P, HALF], F32)
+        nc.scalar.activation(out=sq1[:], in_=u1[:, 512:1024], func=ACT.Square)
+        xg0 = tile("xg0", [P, J], BF16)
+        nc.vector.tensor_copy(xg0[:], x_raw[0][:].indirect(offs_t[:]))
+        xt_ps0 = ps.tile([P, 2, P], F32, name="xt_ps0", tag="a0")
+        for u in range(2):
+            nc.tensor.transpose(xt_ps0[:, u, :], xg0[:].bitcast(F32)[:, u : J // 2 : 2], ident[:])
+        x_b012 = tile("x_b012", [P, 3 * J], BF16)
+        nc.scalar.copy(out=x_b012[:, 0 * J : 1 * J].bitcast(F32).rearrange("q (k u) -> q k u", u=2), in_=xt_ps0[:].rearrange("q u k -> q k u"))
+        ds = tile("ds", [P, U], F32, on="x_raw0")
+        nc.vector.scalar_tensor_tensor(out=ds[:, 0:512], in0=sq0[:], scalar=1.0, in1=c0_0[:], op0=ALU.subtract, op1=ALU.mult)
+        nc.vector.scalar_tensor_tensor(out=ds[:, 512:1024], in0=sq1[:], scalar=1.0, in1=c0_1[:], op0=ALU.subtract, op1=ALU.mult)
         dh1 = tile("dh1", [P, J], F32)
         nc.vector.tensor_copy(dh1[:], ds[:].indirect(offs2_t[:]))
         da = tile("da", [P, PACK, P], F32)
-        nc.scalar.activation(out=da[:].rearrange("r t q -> r q t"), in_=dh1[:].rearrange("r (q t) -> r q t", t=PACK),
-                             func=ACT.Copy, scale=gain_t[:])
-        gt_ps = ps.tile([P, PACK, P], F32, name="gt_ps")
+        nc.scalar.activation(out=da[:].rearrange("r t q -> r q t"), in_=dh1[:].rearrange("r (q t) -> r q t", t=PACK), func=ACT.Copy, scale=gain_t[:])
+        gt_ps = ps.tile([P, PACK, P], F32, name="gt_ps", tag="gt")
         for t in range(PACK):
             nc.tensor.transpose(gt_ps[:, t, :], da[:, t, :], ident[:])
-        gather_x(1)
-        quantize_x(0, "ds")
-        g_b = tile("g_b", [P, R, PACK], BF16)
-        g_c = tile("g_c", [P, R], U32)
+        xg1 = tile("xg1", [P, J], BF16, on="sq1")
+        nc.vector.tensor_copy(xg1[:], x_raw[1][:].indirect(offs_t[:]))
+        xg2 = tile("xg2", [P, J], BF16)
+        nc.vector.tensor_copy(xg2[:], x_raw[2][:].indirect(offs_t[:]))
+        xt_ps2 = ps.tile([P, 2, P], F32, name="xt_ps2", tag="x2")
+        for u in range(2):
+            nc.tensor.transpose(xt_ps2[:, u, :], xg2[:].bitcast(F32)[:, u : J // 2 : 2], ident[:])
+        nc.scalar.copy(out=x_b012[:, 2 * J : 3 * J].bitcast(F32).rearrange("q (k u) -> q k u", u=2), in_=xt_ps2[:].rearrange("q u k -> q k u"))
+        g_b = tile("g_b", [P, R, PACK], BF16, on="x_raw2")
+        nc.vector.tensor_tensor(g_b[:], gt_ps[:].rearrange("q t r -> q r t"), js_t[:].unsqueeze(1).to_broadcast([P, R, PACK]), ALU.mult)
+        xt_ps1 = ps.tile([P, 2, P], F32, name="xt_ps1", tag="gt")
+        for u in range(2):
+            nc.tensor.transpose(xt_ps1[:, u, :], xg1[:].bitcast(F32)[:, u : J // 2 : 2], ident[:])
+        nc.scalar.copy(out=x_b012[:, 1 * J : 2 * J].bitcast(F32).rearrange("q (k u) -> q k u", u=2), in_=xt_ps1[:].rearrange("q u k -> q k u"))
+        xg3 = tile("xg3", [P, J], BF16)
+        nc.vector.tensor_copy(xg3[:], x_raw[3][:].indirect(offs_t[:]))
+        xt_ps3 = ps.tile([P, 2, P], F32, name="xt_ps3", tag="x3")
+        for u in range(2):
+            nc.tensor.transpose(xt_ps3[:, u, :], xg3[:].bitcast(F32)[:, u : J // 2 : 2], ident[:])
+        x_b3 = tile("x_b3", [P, J], BF16)
+        nc.scalar.copy(out=x_b3[:].bitcast(F32).rearrange("q (k u) -> q k u", u=2), in_=xt_ps3[:].rearrange("q u k -> q k u"))
+        last_c = tile("last_c", [P, R + 3 * P], U32, on="x_raw3")
+        g_c = last_c[:, 0:R]
         g_s = tile("g_s", [P, R], U8)
-        nc.vector.tensor_tensor(g_b[:], gt_ps[:].rearrange("q t r -> q r t"),
-                                js_t[:].unsqueeze(1).to_broadcast([P, R, PACK]), ALU.mult)
-        quantize_x(1, None)
-        quantize(nc, g_c[:], g_s[:], g_b[:].rearrange("q r t -> q (r t)"))
-        gather_x(2)
-        gather_x(3)
-        quantize_x(2, "x_raw3")
-
-        out_rows = out.rearrange("(p t) r -> p t r", t=PACK)
-        gw_a = ps.tile([P, PACK - 1, R], F32, name="gw_a")
-        gw_b = ps.tile([P, 1, R], F32, name="gw_b")
-        y_a = tile("y_a", [P, PACK - 1, R], F32)
+        x_s012 = tile("x_s012", [P, 3 * P], U8)
+        quantize(nc, g_c, g_s[:], g_b[:].rearrange("q r t -> q (r t)"))
+        quantize(nc, last_c[:, R : R + 2 * P], x_s012[:, 0 : 2 * P], x_b012[:, 0 : 2 * J])
+        quantize(nc, last_c[:, R + 2 * P : R + 3 * P], x_s012[:, 2 * P : 3 * P], x_b012[:, 2 * J : 3 * J])
+        x_c0, x_c1, x_c2 = [last_c[:, R + t * P : R + (t + 1) * P] for t in range(3)]
+        x_s0, x_s1, x_s2 = [x_s012[:, t * P : (t + 1) * P] for t in range(3)]
+        gw_a = ps.tile([P, 3, R], F32, name="gw_a", tag="c0")
+        nc.tensor.matmul_mx(out=gw_a[:, 0, :], lhsT=x_c0[:].bitcast(FP8X4), lhsT_scale=x_s0[:], rhs=g_c[:].bitcast(FP8X4), rhs_scale=g_s[:], start=True, stop=True)
+        nc.tensor.matmul_mx(out=gw_a[:, 1, :], lhsT=x_c1[:].bitcast(FP8X4), lhsT_scale=x_s1[:], rhs=g_c[:].bitcast(FP8X4), rhs_scale=g_s[:], start=True, stop=True)
+        nc.tensor.matmul_mx(out=gw_a[:, 2, :], lhsT=x_c2[:].bitcast(FP8X4), lhsT_scale=x_s2[:], rhs=g_c[:].bitcast(FP8X4), rhs_scale=g_s[:], start=True, stop=True)
+        x_c3 = tile("x_c3", [P, P], U32)
+        x_s3 = tile("x_s3", [P, P], U8)
+        quantize(nc, x_c3[:], x_s3[:], x_b3[:])
+        y_a = tile("y_a", [P, 3, R], F32, on="x_b3")
+        nc.vector.tensor_tensor(y_a[:], gw_a[:], old_t[:, 0:3, :], ALU.add)
+        nc.sync.dma_start(out=out.rearrange("(p t) r -> p t r", t=PACK)[:, 0:3, :], in_=y_a[:])
+        gw_b = ps.tile([P, 1, R], F32, name="gw_b", tag="c1")
+        nc.tensor.matmul_mx(out=gw_b[:, 0, :], lhsT=x_c3[:].bitcast(FP8X4), lhsT_scale=x_s3[:], rhs=g_c[:].bitcast(FP8X4), rhs_scale=g_s[:], start=True, stop=True)
         y_b = tile("y_b", [P, 1, R], F32)
-        for t in range(PACK - 1):
-            nc.tensor.matmul_mx(out=gw_a[:, t, :], lhsT=x_c[t][:].bitcast(FP8X4), lhsT_scale=x_s[t][:],
-                                rhs=g_c[:].bitcast(FP8X4), rhs_scale=g_s[:], start=True, stop=True)
-        nc.vector.tensor_tensor(y_a[:], gw_a[:], old_t[:, 0 : PACK - 1, :], ALU.add)
-        nc.sync.dma_start(out=out_rows[:, 0 : PACK - 1, :], in_=y_a[:])
-        t = PACK - 1
-        quantize_x(t, None)
-        nc.tensor.matmul_mx(out=gw_b[:, 0, :], lhsT=x_c[t][:].bitcast(FP8X4), lhsT_scale=x_s[t][:],
-                            rhs=g_c[:].bitcast(FP8X4), rhs_scale=g_s[:], start=True, stop=True)
-        nc.vector.tensor_tensor(y_b[:], gw_b[:], old_t[:, t : t + 1, :], ALU.add)
-        nc.sync.dma_start(out=out_rows[:, t : t + 1, :], in_=y_b[:])
+        nc.vector.tensor_tensor(y_b[:], gw_b[:], old_t[:, 3:4, :], ALU.add)
+        nc.sync.dma_start(out=out.rearrange("(p t) r -> p t r", t=PACK)[:, 3:4, :], in_=y_b[:])

@@ -62,8 +62,7 @@ def tile_attend_cpageput_w_kernel(tc, tab_words, tab_scales, w1, gain, ground, w
 
         nc.vector.memset(tab_s[:].bitcast(I32), 0)
         nc.vector.memset(page[:], 0.0)
-        nc.gpsimd.dma_start(out=gain_t[:], in_=gain)
-        nc.gpsimd.dma_start(out=js_t[:], in_=js.rearrange("o (q t) -> (o q) t", t=PACK))
+        nc.scalar.dma_start(out=gain_t[:], in_=gain)
         make_identity(nc, ident[:])
 
         x_planes = xrows.rearrange("(p t) c -> p t c", t=PACK)
@@ -75,6 +74,7 @@ def tile_attend_cpageput_w_kernel(tc, tab_words, tab_scales, w1, gain, ground, w
         nc.sync.dma_start(out=w1_raw[:], in_=w1.rearrange("(p t) r -> p t r", t=PACK))
         nc.sync.dma_start(out=wo_raw[:], in_=wo.rearrange("(p t) r -> p t r", t=PACK))
         nc.sync.dma_start(out=dy_raw[0][:], in_=dy_rows[:, :, 0:256])
+        nc.sync.dma_start(out=js_t[:], in_=js.rearrange("o (q t) -> (o q) t", t=PACK))
         nc.sync.dma_start(offs2_t[:], offs2)
         nc.sync.dma_start(out=dy_raw[1][:], in_=dy_rows[:, :, 256:512])
         nc.sync.dma_start(out=dy_raw[2][:], in_=dy_rows[:, :, 512:768])
@@ -100,6 +100,8 @@ def tile_attend_cpageput_w_kernel(tc, tab_words, tab_scales, w1, gain, ground, w
         nc.tensor.matmul_mx(out=a_ps0[:], lhsT=w1_c[:].bitcast(FP8X4), lhsT_scale=w1_s[:], rhs=tabg_w0[:].bitcast(FP4X4), rhs_scale=tabg_s0[:], start=True, stop=True)
         h1_0 = tile("h1_0", [P, 256], F32)
         nc.scalar.activation(out=h1_0[:], in_=a_ps0[:], func=ACT.Copy, scale=gain_t[:])
+        dy_b0 = tile("dy_b0", [P, HALF, PACK], BF16)
+        interleave(nc, dy_b0[:, 0:256, :], dy_raw[0][:], 1.0)
         tabg_s1 = tile("tabg_s1", [P, 256], U8, on="w1_raw")
         nc.vector.tensor_copy(tabg_s1[:], tab_s[:].indirect(offs_t[:, slice(16, 32)]))
         tabg_w1 = tile("tabg_w1", [P, 256], U16, on="w1_b")
@@ -108,8 +110,6 @@ def tile_attend_cpageput_w_kernel(tc, tab_words, tab_scales, w1, gain, ground, w
         nc.tensor.matmul_mx(out=a_ps1[:], lhsT=w1_c[:].bitcast(FP8X4), lhsT_scale=w1_s[:], rhs=tabg_w1[:].bitcast(FP4X4), rhs_scale=tabg_s1[:], start=True, stop=True)
         h1_1 = tile("h1_1", [P, 256], F32)
         nc.scalar.activation(out=h1_1[:], in_=a_ps1[:], func=ACT.Copy, scale=gain_t[:])
-        dy_b0 = tile("dy_b0", [P, HALF, PACK], BF16)
-        interleave(nc, dy_b0[:, 0:256, :], dy_raw[0][:], 1.0)
         wo_c = tile("wo_c", [P, R], U32)
         wo_s = tile("wo_s", [P, R], U8)
         quantize(nc, wo_c[:], wo_s[:], wo_b[:].rearrange("p r t -> p (r t)"))
@@ -119,6 +119,11 @@ def tile_attend_cpageput_w_kernel(tc, tab_words, tab_scales, w1, gain, ground, w
         dy_b1 = tile("dy_b1", [P, HALF, PACK], BF16)
         interleave(nc, dy_b1[:, 0:256, :], dy_raw[2][:], 1.0)
         interleave(nc, dy_b1[:, 256:512, :], dy_raw[3][:], 1.0)
+        js_ps = ps.tile([P, PACK, P], F32, name="js_ps", tag="a1")
+        for t in range(PACK):
+            nc.tensor.transpose(js_ps[:, t, :], js_t[:, t : t + 1].to_broadcast([P, P]), ident[:])
+        js_row = tile("js_row", [P, J], F32)
+        nc.scalar.copy(out=js_row[:].rearrange("r (q t) -> r q t", t=PACK), in_=js_ps[:].rearrange("r t q -> r q t"))
         dy_c0 = tile("dy_c0", [P, HALF], U32)
         dy_s0 = tile("dy_s0", [P, HALF], U8)
         quantize(nc, dy_c0[:], dy_s0[:], dy_b0[:].rearrange("p u t -> p (u t)"))
@@ -145,32 +150,34 @@ def tile_attend_cpageput_w_kernel(tc, tab_words, tab_scales, w1, gain, ground, w
         xt_ps0 = ps.tile([P, 2, P], F32, name="xt_ps0", tag="a0")
         for u in range(2):
             nc.tensor.transpose(xt_ps0[:, u, :], xg0[:].bitcast(F32)[:, u : J // 2 : 2], ident[:])
-        x_b012 = tile("x_b012", [P, 3 * J], BF16)
-        nc.scalar.copy(out=x_b012[:, 0 * J : 1 * J].bitcast(F32).rearrange("q (k u) -> q k u", u=2), in_=xt_ps0[:].rearrange("q u k -> q k u"))
+        xa_b = tile("xa_b", [P, T], BF16, on="dy_raw3")
+        nc.scalar.activation(out=xa_b[:], in_=x_raw[1][:], func=ACT.Copy)
+        xg1 = tile("xg1", [P, J], BF16)
+        nc.scalar.activation(out=xg1[:], in_=xa_b[:].indirect(offs_t[:]), func=ACT.Copy)
+        xt_ps1 = ps.tile([P, 2, P], F32, name="xt_ps1", tag="gt0")
+        for u in range(2):
+            nc.tensor.transpose(xt_ps1[:, u, :], xg1[:].bitcast(F32)[:, u : J // 2 : 2], ident[:])
         ds = tile("ds", [P, U], F32, on="x_raw0")
         nc.vector.scalar_tensor_tensor(out=ds[:, 0:512], in0=sq0[:], scalar=1.0, in1=c0_0[:], op0=ALU.subtract, op1=ALU.mult)
         nc.vector.scalar_tensor_tensor(out=ds[:, 512:1024], in0=sq1[:], scalar=1.0, in1=c0_1[:], op0=ALU.subtract, op1=ALU.mult)
         dh1 = tile("dh1", [P, J], F32)
-        nc.vector.tensor_copy(dh1[:], ds[:].indirect(offs2_t[:]))
-        da = tile("da", [P, PACK, P], F32)
-        nc.scalar.activation(out=da[:].rearrange("r t q -> r q t"), in_=dh1[:].rearrange("r (q t) -> r q t", t=PACK), func=ACT.Copy, scale=gain_t[:])
-        gt_ps = ps.tile([P, PACK, P], F32, name="gt_ps", tag="gt")
-        for t in range(PACK):
-            nc.tensor.transpose(gt_ps[:, t, :], da[:, t, :], ident[:])
-        xg1 = tile("xg1", [P, J], BF16, on="sq1")
-        nc.vector.tensor_copy(xg1[:], x_raw[1][:].indirect(offs_t[:]))
+        nc.vector.tensor_tensor(dh1[:], ds[:].indirect(offs2_t[:]), js_row[:], ALU.mult)
+        da = tile("da", [P, J], BF16, on="dy_raw3")
+        nc.scalar.activation(out=da[:], in_=dh1[:], func=ACT.Copy, scale=gain_t[:])
+        gt_ps = ps.tile([P, 2, P], F32, name="gt_ps", tag="gt")
+        for u in range(2):
+            nc.tensor.transpose(gt_ps[:, u, :], da[:].bitcast(F32)[:, u : J // 2 : 2], ident[:])
         xg2 = tile("xg2", [P, J], BF16)
         nc.vector.tensor_copy(xg2[:], x_raw[2][:].indirect(offs_t[:]))
         xt_ps2 = ps.tile([P, 2, P], F32, name="xt_ps2", tag="x2")
         for u in range(2):
             nc.tensor.transpose(xt_ps2[:, u, :], xg2[:].bitcast(F32)[:, u : J // 2 : 2], ident[:])
-        nc.scalar.copy(out=x_b012[:, 2 * J : 3 * J].bitcast(F32).rearrange("q (k u) -> q k u", u=2), in_=xt_ps2[:].rearrange("q u k -> q k u"))
-        g_b = tile("g_b", [P, R, PACK], BF16, on="x_raw2")
-        nc.vector.tensor_tensor(g_b[:], gt_ps[:].rearrange("q t r -> q r t"), js_t[:].unsqueeze(1).to_broadcast([P, R, PACK]), ALU.mult)
-        xt_ps1 = ps.tile([P, 2, P], F32, name="xt_ps1", tag="gt")
-        for u in range(2):
-            nc.tensor.transpose(xt_ps1[:, u, :], xg1[:].bitcast(F32)[:, u : J // 2 : 2], ident[:])
+        x_b012 = tile("x_b012", [P, 3 * J], BF16, on="dh1")
+        nc.scalar.copy(out=x_b012[:, 0 * J : 1 * J].bitcast(F32).rearrange("q (k u) -> q k u", u=2), in_=xt_ps0[:].rearrange("q u k -> q k u"))
         nc.scalar.copy(out=x_b012[:, 1 * J : 2 * J].bitcast(F32).rearrange("q (k u) -> q k u", u=2), in_=xt_ps1[:].rearrange("q u k -> q k u"))
+        g_b = tile("g_b", [P, R, PACK], BF16)
+        nc.scalar.copy(out=g_b[:].rearrange("q r t -> q (r t)").bitcast(F32).rearrange("q (r u) -> q r u", u=2), in_=gt_ps[:].rearrange("q u r -> q r u"))
+        nc.scalar.copy(out=x_b012[:, 2 * J : 3 * J].bitcast(F32).rearrange("q (k u) -> q k u", u=2), in_=xt_ps2[:].rearrange("q u k -> q k u"))
         xg3 = tile("xg3", [P, J], BF16)
         nc.vector.tensor_copy(xg3[:], x_raw[3][:].indirect(offs_t[:]))
         xt_ps3 = ps.tile([P, 2, P], F32, name="xt_ps3", tag="x3")
@@ -182,9 +189,9 @@ def tile_attend_cpageput_w_kernel(tc, tab_words, tab_scales, w1, gain, ground, w
         g_c = last_c[:, 0:R]
         g_s = tile("g_s", [P, R], U8)
         x_s012 = tile("x_s012", [P, 3 * P], U8)
-        quantize(nc, g_c, g_s[:], g_b[:].rearrange("q r t -> q (r t)"))
         quantize(nc, last_c[:, R : R + 2 * P], x_s012[:, 0 : 2 * P], x_b012[:, 0 : 2 * J])
         quantize(nc, last_c[:, R + 2 * P : R + 3 * P], x_s012[:, 2 * P : 3 * P], x_b012[:, 2 * J : 3 * J])
+        quantize(nc, g_c, g_s[:], g_b[:].rearrange("q r t -> q (r t)"))
         x_c0, x_c1, x_c2 = [last_c[:, R + t * P : R + (t + 1) * P] for t in range(3)]
         x_s0, x_s1, x_s2 = [x_s012[:, t * P : (t + 1) * P] for t in range(3)]
         gw_a = ps.tile([P, 3, R], F32, name="gw_a", tag="c0")

from contextlib import ExitStack

import concourse.mybir as mybir
from concourse.masks import make_identity

K, R, F, T, J, U = 512, 128, 512, 2048, 512, 1024
FLOPS = 2 * K * R * J + 2 * F * R * U + 2 * J * K * R

F32 = mybir.dt.float32
BF16 = mybir.dt.bfloat16
I32 = mybir.dt.int32
U32 = mybir.dt.uint32
U16 = mybir.dt.uint16
U8 = mybir.dt.uint8
FP8X4 = mybir.dt.float8_e4m3fn_x4
FP4X4 = mybir.dt.float4_e2m1fn_x4
ACT = mybir.ActivationFunctionType
ALU = mybir.AluOpType

P = 128
PACK = 4
HALF = U // 2


def interleave(nc, grouped, raw, scale):
    nc.scalar.activation(
        out=grouped.rearrange("p (c i) t -> p c t i", i=4),
        in_=raw.rearrange("p t (c i) -> p c t i", i=4),
        func=ACT.Copy,
        scale=scale,
    )


def quantize(nc, codes, scales, grouped):
    nc.vector.quantize_mx(out=codes.bitcast(FP8X4), scales=scales, in_=grouped)


def tile_attend_cpageput_w_kernel(tc, tab_words, tab_scales, w1, gain, ground, wo, dy, js, xrows, old, offs, offs2, out):
    nc = tc.nc
    with ExitStack() as ctx:
        sb = ctx.enter_context(tc.tile_pool(name="sb", bufs=1))
        ps = ctx.enter_context(tc.psum_pool(name="ps", bufs=1))

        def tile(name, shape, dtype, on=None):
            return sb.tile(shape, dtype, name=name, tag=on or name, align_bytes=64)

        offs_t = sb.tile([P, J // 16], U16, name="offs_t")
        offs2_t = sb.tile([P, J // 16], U16, name="offs2_t")
        tab_w = tile("tab_w", [P, T], U16)
        tab_s = tile("tab_s", [P, T], U8)
        w1_raw = tile("w1_raw", [P, PACK, R], F32)
        wo_raw = tile("wo_raw", [P, PACK, R], F32)
        gain_t = tile("gain_t", [P, 1], F32)
        js_t = tile("js_t", [P, PACK], F32)
        ground_t = tile("ground_t", [P, U], F32)
        dy_cuts = [(0, 256), (256, 512), (512, 768), (768, 1024)]
        dy_raw = [tile("dy_raw%d" % i, [P, PACK, b - a], F32) for i, (a, b) in enumerate(dy_cuts)]
        x_raw = [tile("x_raw%d" % t, [P, T], F32) for t in range(PACK)]
        old_t = tile("old_t", [P, PACK, R], F32)
        ident = tile("ident", [P, P], F32)
        page = tile("page", [P, U], F32)

        nc.vector.memset(tab_s[:].bitcast(I32), 0)
        nc.vector.memset(page[:], 0.0)
        nc.scalar.dma_start(out=gain_t[:], in_=gain)
        make_identity(nc, ident[:])

        x_planes = xrows.rearrange("(p t) c -> p t c", t=PACK)
        dy_rows = dy.rearrange("(p t) u -> p t u", t=PACK)
        nc.sync.dma_start(offs_t[:], offs)
        nc.sync.dma_start(out=tab_w[:].bitcast(I32), in_=tab_words[0].bitcast(I32))
        for i in range(4):
            nc.sync.dma_start(out=tab_s[i:P:32, :].bitcast(I32), in_=tab_scales[0, i:16:4, :].bitcast(I32))
        nc.sync.dma_start(out=w1_raw[:], in_=w1.rearrange("(p t) r -> p t r", t=PACK))
        nc.sync.dma_start(out=wo_raw[:], in_=wo.rearrange("(p t) r -> p t r", t=PACK))
        nc.sync.dma_start(out=dy_raw[0][:], in_=dy_rows[:, :, 0:256])
        nc.sync.dma_start(out=js_t[:], in_=js.rearrange("o (q t) -> (o q) t", t=PACK))
        nc.sync.dma_start(offs2_t[:], offs2)
        nc.sync.dma_start(out=dy_raw[1][:], in_=dy_rows[:, :, 256:512])
        nc.sync.dma_start(out=dy_raw[2][:], in_=dy_rows[:, :, 512:768])
        nc.sync.dma_start(out=dy_raw[3][:], in_=dy_rows[:, :, 768:1024])
        nc.sync.dma_start(out=ground_t[:], in_=ground)
        nc.sync.dma_start(out=x_raw[0][:], in_=x_planes[:, 0, :])
        nc.sync.dma_start(out=x_raw[1][:], in_=x_planes[:, 1, :])
        nc.sync.dma_start(out=x_raw[2][:], in_=x_planes[:, 2, :])
        nc.sync.dma_start(out=x_raw[3][:], in_=x_planes[:, 3, :])
        nc.sync.dma_start(out=old_t[:], in_=old.rearrange("(p t) r -> p t r", t=PACK))
        w1_b = tile("w1_b", [P, R, PACK], BF16)
        interleave(nc, w1_b[:], w1_raw[:], 1.0)
        wo_b = tile("wo_b", [P, R, PACK], BF16)
        interleave(nc, wo_b[:], wo_raw[:], -1.0)
        tabg_w0 = tile("tabg_w0", [P, 256], U16)
        nc.vector.tensor_copy(tabg_w0[:], tab_w[:].indirect(offs_t[:, slice(0, 16)]))
        tabg_s0 = tile("tabg_s0", [P, 256], U8)
        nc.vector.tensor_copy(tabg_s0[:], tab_s[:].indirect(offs_t[:, slice(0, 16)]))
        w1_c = tile("w1_c", [P, R], U32)
        w1_s = tile("w1_s", [P, R], U8)
        quantize(nc, w1_c[:], w1_s[:], w1_b[:].rearrange("p r t -> p (r t)"))
        a_ps0 = ps.tile([P, 256], F32, name="a_ps0", tag="a0")
        nc.tensor.matmul_mx(out=a_ps0[:], lhsT=w1_c[:].bitcast(FP8X4), lhsT_scale=w1_s[:], rhs=tabg_w0[:].bitcast(FP4X4), rhs_scale=tabg_s0[:], start=True, stop=True)
        h1_0 = tile("h1_0", [P, 256], F32)
        nc.scalar.activation(out=h1_0[:], in_=a_ps0[:], func=ACT.Copy, scale=gain_t[:])
        dy_b0 = tile("dy_b0", [P, HALF, PACK], BF16)
        interleave(nc, dy_b0[:, 0:256, :], dy_raw[0][:], 1.0)
        tabg_s1 = tile("tabg_s1", [P, 256], U8, on="w1_raw")
        nc.vector.tensor_copy(tabg_s1[:], tab_s[:].indirect(offs_t[:, slice(16, 32)]))
        tabg_w1 = tile("tabg_w1", [P, 256], U16, on="w1_b")
        nc.vector.tensor_copy(tabg_w1[:], tab_w[:].indirect(offs_t[:, slice(16, 32)]))
        a_ps1 = ps.tile([P, 256], F32, name="a_ps1", tag="a1")
        nc.tensor.matmul_mx(out=a_ps1[:], lhsT=w1_c[:].bitcast(FP8X4), lhsT_scale=w1_s[:], rhs=tabg_w1[:].bitcast(FP4X4), rhs_scale=tabg_s1[:], start=True, stop=True)
        h1_1 = tile("h1_1", [P, 256], F32)
        nc.scalar.activation(out=h1_1[:], in_=a_ps1[:], func=ACT.Copy, scale=gain_t[:])
        wo_c = tile("wo_c", [P, R], U32)
        wo_s = tile("wo_s", [P, R], U8)
        quantize(nc, wo_c[:], wo_s[:], wo_b[:].rearrange("p r t -> p (r t)"))
        nc.vector.tensor_copy(page[:].indirect(offs2_t[:, slice(0, 16)]), h1_0[:])
        nc.vector.tensor_copy(page[:].indirect(offs2_t[:, slice(16, 32)]), h1_1[:])
        interleave(nc, dy_b0[:, 256:512, :], dy_raw[1][:], 1.0)
        dy_b1 = tile("dy_b1", [P, HALF, PACK], BF16)
        interleave(nc, dy_b1[:, 0:256, :], dy_raw[2][:], 1.0)
        interleave(nc, dy_b1[:, 256:512, :], dy_raw[3][:], 1.0)
        js_ps = ps.tile([P, PACK, P], F32, name="js_ps", tag="a1")
        for t in range(PACK):
            nc.tensor.transpose(js_ps[:, t, :], js_t[:, t : t + 1].to_broadcast([P, P]), ident[:])
        js_row = tile("js_row", [P, J], F32)
        nc.scalar.copy(out=js_row[:].rearrange("r (q t) -> r q t", t=PACK), in_=js_ps[:].rearrange("r t q -> r q t"))
        dy_c0 = tile("dy_c0", [P, HALF], U32)
        dy_s0 = tile("dy_s0", [P, HALF], U8)
        quantize(nc, dy_c0[:], dy_s0[:], dy_b0[:].rearrange("p u t -> p (u t)"))
        c0_0 = ps.tile([P, HALF], F32, name="c0_0", tag="c0")
        nc.tensor.matmul_mx(out=c0_0[:], lhsT=wo_c[:].bitcast(FP8X4), lhsT_scale=wo_s[:], rhs=dy_c0[:].bitcast(FP8X4), rhs_scale=dy_s0[:], start=True, stop=True)
        s_t0 = tile("s_t0", [P, HALF], F32)
        nc.vector.tensor_tensor(s_t0[:], page[:, 0:512], ground_t[:, 0:512], ALU.add)
        s_t1 = tile("s_t1", [P, HALF], F32)
        nc.vector.tensor_tensor(s_t1[:], page[:, 512:1024], ground_t[:, 512:1024], ALU.add)
        dy_c1 = tile("dy_c1", [P, HALF], U32)
        dy_s1 = tile("dy_s1", [P, HALF], U8)
        quantize(nc, dy_c1[:], dy_s1[:], dy_b1[:].rearrange("p u t -> p (u t)"))
        c0_1 = ps.tile([P, HALF], F32, name="c0_1", tag="c1")
        nc.tensor.matmul_mx(out=c0_1[:], lhsT=wo_c[:].bitcast(FP8X4), lhsT_scale=wo_s[:], rhs=dy_c1[:].bitcast(FP8X4), rhs_scale=dy_s1[:], start=True, stop=True)
        u1 = tile("u1", [P, U], F32, on="dy_raw3")
        nc.scalar.activation(out=u1[:, 0:512], in_=s_t0[:], func=ACT.Tanh)
        nc.scalar.activation(out=u1[:, 512:1024], in_=s_t1[:], func=ACT.Tanh)
        sq0 = tile("sq0", [P, HALF], F32)
        nc.scalar.activation(out=sq0[:], in_=u1[:, 0:512], func=ACT.Square)
        sq1 = tile("sq1", [P, HALF], F32)
        nc.scalar.activation(out=sq1[:], in_=u1[:, 512:1024], func=ACT.Square)
        xg0 = tile("xg0", [P, J], BF16)
        nc.vector.tensor_copy(xg0[:], x_raw[0][:].indirect(offs_t[:]))
        xt_ps0 = ps.tile([P, 2, P], F32, name="xt_ps0", tag="a0")
        for u in range(2):
            nc.tensor.transpose(xt_ps0[:, u, :], xg0[:].bitcast(F32)[:, u : J // 2 : 2], ident[:])
        xa_b = tile("xa_b", [P, T], BF16, on="dy_raw3")
        nc.scalar.activation(out=xa_b[:], in_=x_raw[1][:], func=ACT.Copy)
        xg1 = tile("xg1", [P, J], BF16)
        nc.scalar.activation(out=xg1[:], in_=xa_b[:].indirect(offs_t[:]), func=ACT.Copy)
        xt_ps1 = ps.tile([P, 2, P], F32, name="xt_ps1", tag="gt0")
        for u in range(2):
            nc.tensor.transpose(xt_ps1[:, u, :], xg1[:].bitcast(F32)[:, u : J // 2 : 2], ident[:])
        ds = tile("ds", [P, U], F32, on="x_raw0")
        nc.vector.scalar_tensor_tensor(out=ds[:, 0:512], in0=sq0[:], scalar=1.0, in1=c0_0[:], op0=ALU.subtract, op1=ALU.mult)
        nc.vector.scalar_tensor_tensor(out=ds[:, 512:1024], in0=sq1[:], scalar=1.0, in1=c0_1[:], op0=ALU.subtract, op1=ALU.mult)
        dh1 = tile("dh1", [P, J], F32)
        nc.vector.tensor_tensor(dh1[:], ds[:].indirect(offs2_t[:]), js_row[:], ALU.mult)
        da = tile("da", [P, J], BF16, on="dy_raw3")
        nc.scalar.activation(out=da[:], in_=dh1[:], func=ACT.Copy, scale=gain_t[:])
        gt_ps = ps.tile([P, 2, P], F32, name="gt_ps", tag="gt")
        for u in range(2):
            nc.tensor.transpose(gt_ps[:, u, :], da[:].bitcast(F32)[:, u : J // 2 : 2], ident[:])
        xg2 = tile("xg2", [P, J], BF16)
        nc.vector.tensor_copy(xg2[:], x_raw[2][:].indirect(offs_t[:]))
        xt_ps2 = ps.tile([P, 2, P], F32, name="xt_ps2", tag="x2")
        for u in range(2):
            nc.tensor.transpose(xt_ps2[:, u, :], xg2[:].bitcast(F32)[:, u : J // 2 : 2], ident[:])
        x_b012 = tile("x_b012", [P, 3 * J], BF16, on="dh1")
        nc.scalar.copy(out=x_b012[:, 0 * J : 1 * J].bitcast(F32).rearrange("q (k u) -> q k u", u=2), in_=xt_ps0[:].rearrange("q u k -> q k u"))
        nc.scalar.copy(out=x_b012[:, 1 * J : 2 * J].bitcast(F32).rearrange("q (k u) -> q k u", u=2), in_=xt_ps1[:].rearrange("q u k -> q k u"))
        g_b = tile("g_b", [P, R, PACK], BF16)
        nc.scalar.copy(out=g_b[:].rearrange("q r t -> q (r t)").bitcast(F32).rearrange("q (r u) -> q r u", u=2), in_=gt_ps[:].rearrange("q u r -> q r u"))
        nc.scalar.copy(out=x_b012[:, 2 * J : 3 * J].bitcast(F32).rearrange("q (k u) -> q k u", u=2), in_=xt_ps2[:].rearrange("q u k -> q k u"))
        xg3 = tile("xg3", [P, J], BF16)
        nc.vector.tensor_copy(xg3[:], x_raw[3][:].indirect(offs_t[:]))
        xt_ps3 = ps.tile([P, 2, P], F32, name="xt_ps3", tag="x3")
        for u in range(2):
            nc.tensor.transpose(xt_ps3[:, u, :], xg3[:].bitcast(F32)[:, u : J // 2 : 2], ident[:])
        x_b3 = tile("x_b3", [P, J], BF16)
        nc.scalar.copy(out=x_b3[:].bitcast(F32).rearrange("q (k u) -> q k u", u=2), in_=xt_ps3[:].rearrange("q u k -> q k u"))
        last_c = tile("last_c", [P, R + 3 * P], U32, on="x_raw3")
        g_c = last_c[:, 0:R]
        g_s = tile("g_s", [P, R], U8)
        x_s012 = tile("x_s012", [P, 3 * P], U8)
        quantize(nc, last_c[:, R : R + 2 * P], x_s012[:, 0 : 2 * P], x_b012[:, 0 : 2 * J])
        quantize(nc, last_c[:, R + 2 * P : R + 3 * P], x_s012[:, 2 * P : 3 * P], x_b012[:, 2 * J : 3 * J])
        quantize(nc, g_c, g_s[:], g_b[:].rearrange("q r t -> q (r t)"))
        x_c0, x_c1, x_c2 = [last_c[:, R + t * P : R + (t + 1) * P] for t in range(3)]
        x_s0, x_s1, x_s2 = [x_s012[:, t * P : (t + 1) * P] for t in range(3)]
        gw_a = ps.tile([P, 3, R], F32, name="gw_a", tag="c0")
        nc.tensor.matmul_mx(out=gw_a[:, 0, :], lhsT=x_c0[:].bitcast(FP8X4), lhsT_scale=x_s0[:], rhs=g_c[:].bitcast(FP8X4), rhs_scale=g_s[:], start=True, stop=True)
        nc.tensor.matmul_mx(out=gw_a[:, 1, :], lhsT=x_c1[:].bitcast(FP8X4), lhsT_scale=x_s1[:], rhs=g_c[:].bitcast(FP8X4), rhs_scale=g_s[:], start=True, stop=True)
        nc.tensor.matmul_mx(out=gw_a[:, 2, :], lhsT=x_c2[:].bitcast(FP8X4), lhsT_scale=x_s2[:], rhs=g_c[:].bitcast(FP8X4), rhs_scale=g_s[:], start=True, stop=True)
        x_c3 = tile("x_c3", [P, P], U32)
        x_s3 = tile("x_s3", [P, P], U8)
        quantize(nc, x_c3[:], x_s3[:], x_b3[:])
        y_a = tile("y_a", [P, 3, R], F32, on="x_b3")
        nc.vector.tensor_tensor(y_a[:], gw_a[:], old_t[:, 0:3, :], ALU.add)
        nc.sync.dma_start(out=out.rearrange("(p t) r -> p t r", t=PACK)[:, 0:3, :], in_=y_a[:])
        gw_b = ps.tile([P, 1, R], F32, name="gw_b", tag="c1")
        nc.tensor.matmul_mx(out=gw_b[:, 0, :], lhsT=x_c3[:].bitcast(FP8X4), lhsT_scale=x_s3[:], rhs=g_c[:].bitcast(FP8X4), rhs_scale=g_s[:], start=True, stop=True)
        y_b = tile("y_b", [P, 1, R], F32)
        nc.vector.tensor_tensor(y_b[:], gw_b[:], old_t[:, 3:4, :], ALU.add)
        nc.sync.dma_start(out=out.rearrange("(p t) r -> p t r", t=PACK)[:, 3:4, :], in_=y_b[:])
